import numpy as np
import ml_dtypes


def mxq(x, axis, fmt="e4m3"):
    dtype, down = {"e4m3": (ml_dtypes.float8_e4m3fn, 7), "e5m2": (ml_dtypes.float8_e5m2, 14)}[fmt]
    v = np.moveaxis(np.asarray(x, np.float32).astype(ml_dtypes.bfloat16).astype(np.float64), axis, -1)
    blocks = v.reshape(v.shape[:-1] + (-1, 32))
    amax = np.abs(blocks).max(-1, keepdims=True)
    byte = np.maximum(np.where(amax > 0, np.frexp(amax)[1] - 1 + 127, 0) - down, 1)
    scale = np.exp2(byte - 127.0)
    codes = (blocks / scale).astype(np.float32).astype(dtype).astype(np.float64)
    return np.moveaxis((codes * scale).reshape(v.shape), -1, axis)


WIDE = False


def mx_kscale(k):
    if not WIDE:
        return np.ones(k)
    levels = np.array([24, -24, 12, -12, 0])
    if k % 512:
        return np.exp2(np.random.permutation(np.resize(levels, k // 32))).repeat(32)
    a = np.empty((k // 512, 16))
    for p in range(k // 512):
        a[p, :8] = np.random.permutation(np.resize(levels, 8))
        for g in range(8):
            far = levels[np.abs(levels - a[p, g]) >= 10]
            a[p, g + 8] = far[np.random.randint(len(far))]
    return np.exp2(a.ravel()).repeat(32)


def f64(x):
    return np.asarray(x).astype(np.float64)


def striped(idx):
    return np.tile(idx.reshape(-1, 16).T, (8, 1)).astype(np.uint16)


def unstriped(offs):
    return offs[:16].T.reshape(-1).astype(np.int64)


def striped8(idx):
    return np.concatenate([v.reshape(-1, 16).T for v in idx]).astype(np.uint16)


def unstriped8(offs):
    return np.stack([offs[16 * g:16 * g + 16].T.reshape(-1) for g in range(8)]).astype(np.int64)


E2M1 = np.array([0.0, 0.5, 1.0, 1.5, 2.0, 3.0, 4.0, 6.0, -0.0, -0.5, -1.0, -1.5, -2.0, -3.0, -4.0, -6.0])


def pack_weight(w, fmt):
    k, n = w.shape
    w = f64(np.asarray(w, np.float32).astype(ml_dtypes.bfloat16)).reshape(k // 32, 32, n)
    amax = np.abs(w).max(1)
    if fmt == "e4m3":
        byte = np.frexp(amax)[1] - 1 + 127 - 7
    else:
        mant, ex = np.frexp(amax / 6.0)
        byte = np.where(mant > 0.5, ex, ex - 1) + 127
    byte = np.clip(np.where(amax > 0, byte, 1), 1, 254)
    scaled = (w * np.exp2(127.0 - byte)[:, None, :]).reshape(k, n).astype(np.float32)
    by_word = np.ascontiguousarray(scaled.reshape(k // 512, 128, 4, n).transpose(0, 1, 3, 2))
    if fmt == "e4m3":
        words = by_word.astype(ml_dtypes.float8_e4m3fn).view(np.uint8)
    else:
        c = by_word.astype(ml_dtypes.float4_e2m1fn).view(np.uint8) & 0xF
        words = (c[..., 0::2] | (c[..., 1::2] << 4)).reshape(k // 512, 128, 2 * n)
    return np.ascontiguousarray(words), np.ascontiguousarray(byte.astype(np.uint8).reshape(k // 512, 16, n))


def unpack_weight(words, scales, fmt):
    g, _, n = scales.shape
    words = np.ascontiguousarray(words).reshape(g, 128, n, -1)
    if fmt == "e4m3":
        vals = words.view(ml_dtypes.float8_e4m3fn).astype(np.float64)
    else:
        nib = np.empty((g, 128, n, 4), np.uint8)
        nib[..., 0::2] = words & 0xF
        nib[..., 1::2] = words >> 4
        vals = E2M1[nib]
    vals = vals * np.repeat(np.exp2(scales.astype(np.float64) - 127.0), 8, axis=1)[..., None]
    return vals.transpose(0, 1, 3, 2).reshape(g * 512, n)


def silu(f):
    return f / (1.0 + np.exp(-np.maximum(f, -700.0)))


K, L, R, N, T, J = 512, 512, 512, 512, 2048, 1024


def setup_inputs():
    n = np.random.standard_normal
    s = mx_kscale(K)[:, None]
    s2 = mx_kscale(L)[:, None]
    u = mx_kscale(R)[:, None]
    p_tab = pack_weight(n((L, T)) * s2, "e4m3")
    p_wb = pack_weight(n((L, R)) / np.sqrt(L) / s2 * u.T, "e4m3")
    p_wd = pack_weight(n((R, N)) / np.sqrt(R) / u, "e4m3")
    return {
        "tab_words": p_tab[0],
        "tab_scales": p_tab[1],
        "xT": (n((K, T)) * s).astype(np.float32),
        "wgt2": np.repeat(np.random.uniform(0.5, 2.0, (8, J)), 16, axis=0).astype(np.float32),
        "wa": (n((K, R)) / np.sqrt(K) / s).astype(np.float32),
        "wb_words": p_wb[0],
        "wb_scales": p_wb[1],
        "wd_words": p_wd[0],
        "wd_scales": p_wd[1],
        "offs": striped(np.random.permutation(T)[:J]),
        "offs2": striped8(np.stack([np.random.permutation(T)[:J] for _ in range(8)])),
    }


def reference(tab_words, tab_scales, xT, wgt2, wa, wb_words, wb_scales, wd_words, wd_scales, offs, offs2):
    idx = unstriped(offs)
    idx2 = unstriped8(offs2)
    tab_ = unpack_weight(tab_words, tab_scales, "e4m3")[:, idx]
    rows = np.arange(K)
    xg = f64(wgt2)[rows // 4 % 128] * f64(xT)[rows[:, None], idx2[rows % 512 // 64]]
    xT_ = mxq(xg, 0, "e4m3")
    wa_ = mxq(f64(wa), 0, "e4m3")
    wb_ = unpack_weight(wb_words, wb_scales, "e4m3")
    ya = wa_.T @ xT_
    yb = wb_.T @ tab_
    h = silu(ya) * yb
    h_ = mxq(h, 0, "e4m3")
    wd_ = unpack_weight(wd_words, wd_scales, "e4m3")
    y = wd_.T @ h_
    return y

@@ -1,0 +1,225 @@
+from contextlib import ExitStack
+
+import concourse.mybir as mybir
+
+K, L, R, N, T, J = 512, 512, 512, 512, 2048, 1024
+FLOPS = 2 * J * (K * R + L * R + R * N)
+
+F32 = mybir.dt.float32
+BF16 = mybir.dt.bfloat16
+I32 = mybir.dt.int32
+U32 = mybir.dt.uint32
+U16 = mybir.dt.uint16
+U8 = mybir.dt.uint8
+FP8X4 = mybir.dt.float8_e4m3fn_x4
+MULT = mybir.AluOpType.mult
+SILU = mybir.ActivationFunctionType.Silu
+
+P = 128
+PACK = 4
+LIST_ROWS = 16
+HALF = J // 2
+QUARTER = J // 4
+CHUNK = 128
+
+
+def tile_list_htabg_glu_none_kernel(
+    tc, tab_words, tab_scales, xT, wgt2, wa, wb_words, wb_scales, wd_words, wd_scales, offs, offs2, out
+):
+    nc = tc.nc
+    with ExitStack() as ctx:
+        keep = ctx.enter_context(tc.tile_pool(name="keep", bufs=1))
+        ring = ctx.enter_context(tc.tile_pool(name="ring", bufs=2))
+        psum = ctx.enter_context(tc.psum_pool(name="psum", bufs=2))
+
+        def load_scale_rows(plane, rows):
+            for quad in range(4):
+                nc.sync.dma_start(
+                    plane[32 * quad : 32 * quad + 4, :].bitcast(I32),
+                    rows[0, 4 * quad : 4 * quad + 4, :].bitcast(I32),
+                )
+
+        def load_words(name, words, width):
+            tile = keep.tile([P, width], I32, name=name, align_bytes=64)
+            nc.sync.dma_start(tile[:], words[0].rearrange("p n t -> p (n t)").bitcast(I32))
+            return tile
+
+        def entries(offsets, first, count):
+            return offsets[:, first // LIST_ROWS : (first + count) // LIST_ROWS]
+
+        def product(acc, w_codes, w_plane, codes, plane):
+            nc.tensor.matmul_mx(
+                out=acc,
+                lhsT=w_codes.bitcast(FP8X4),
+                lhsT_scale=w_plane,
+                rhs=codes.bitcast(FP8X4),
+                rhs_scale=plane,
+                start=True,
+                stop=True,
+            )
+
+        tab_list = keep.tile([P, J // LIST_ROWS], U16, name="tab_list")
+        nc.sync.dma_start(tab_list[:], offs)
+        tab_rows = keep.tile([P, T], U8, name="tab_rows", align_bytes=64)
+        nc.sync.dma_start(
+            tab_rows[:].bitcast(I32), tab_scales[0].bitcast(I32).unsqueeze(1).to_broadcast([16, 8, T // 4])
+        )
+        head_lists = keep.tile([P, J // LIST_ROWS], U16, name="head_lists")
+        nc.sync.dma_start(head_lists[:], offs2)
+
+        v_plane = keep.tile([P, J], U8, name="v_plane", align_bytes=64)
+        wb_plane_raw = keep.tile([P, R], U8, name="wb_plane_raw", align_bytes=64)
+        wd_plane = keep.tile([P, N], U8, name="wd_plane", align_bytes=64)
+        for plane in (v_plane, wb_plane_raw, wd_plane):
+            nc.gpsimd.memset(plane[:].bitcast(I32), 0)
+
+        x_rows = xT.rearrange("(p i) t -> p i t", i=PACK)
+        x_planes = [keep.tile([P, T], F32, name="x_plane%d" % i) for i in range(PACK)]
+        wgt = [keep.tile([P, HALF], F32, name="wgt%d" % h) for h in range(2)]
+        wa_raw = keep.tile([P, PACK, R], F32, name="wa_raw")
+
+        nc.sync.dma_start(wgt[0][:], wgt2[:, 0:HALF])
+        nc.sync.dma_start(x_planes[0][:], x_rows[:, 0, :])
+        nc.sync.dma_start(wgt[1][:], wgt2[:, HALF:J])
+        nc.sync.dma_start(x_planes[1][:], x_rows[:, 1, :])
+        v_rows = keep.tile([P, J], U8, name="v_rows", align_bytes=64)
+        nc.vector.tensor_copy(v_rows[:], tab_rows[:].indirect(tab_list[:]))
+        load_scale_rows(wb_plane_raw, wb_scales)
+        nc.sync.dma_start(x_planes[2][:], x_rows[:, 2, :])
+        for quad in range(4):
+            nc.sync.dma_start(
+                v_plane[32 * quad : 32 * quad + 4, :].bitcast(I32),
+                v_rows[32 * quad : 32 * quad + 32 : 8, :].bitcast(I32),
+            )
+        wb_raw = load_words("wb_raw", wb_words, R)
+        nc.sync.dma_start(x_planes[3][:], x_rows[:, 3, :])
+        nc.sync.dma_start(wa_raw[:], wa.rearrange("(p i) r -> p i r", i=PACK))
+        tab = load_words("tab", tab_words, T)
+        wd = load_words("wd", wd_words, N)
+        load_scale_rows(wd_plane, wd_scales)
+
+        warm = keep.tile([P, 1], F32, name="warm")
+        nc.scalar.activation(warm[:], wgt[0][:, 0:1], SILU)
+
+        picked = [keep.tile([P, PACK, HALF], F32, name="picked%d" % h) for h in range(2)]
+        for i in range(PACK - 1):
+            for h in range(2):
+                window = x_planes[i][:].indirect(entries(head_lists, h * HALF, HALF))
+                nc.vector.tensor_tensor(picked[h][:, i, :], window, wgt[h][:], MULT)
+
+        x_codes = [keep.tile([P, QUARTER], U32, name="x_codes%d" % q, align_bytes=64) for q in range(4)]
+        x_scales = [keep.tile([P, QUARTER], U8, name="x_scales%d" % q, align_bytes=64) for q in range(4)]
+        x_bf = [keep.tile([P, PACK * QUARTER], BF16, name="x_bf%d" % q, align_bytes=64) for q in range(4)]
+
+        def quarter_cols(q):
+            return q // 2, slice((q % 2) * QUARTER, (q % 2 + 1) * QUARTER)
+
+        def pick_last_plane(q):
+            h, cols = quarter_cols(q)
+            window = x_planes[PACK - 1][:].indirect(entries(head_lists, q * QUARTER, QUARTER))
+            nc.vector.tensor_tensor(picked[h][:, PACK - 1, cols], window, wgt[h][:, cols], MULT)
+
+        def weave_x(q):
+            h, cols = quarter_cols(q)
+            nc.scalar.copy(
+                x_bf[q][:].rearrange("p (c e i) -> p c i e", e=4, i=PACK),
+                picked[h][:, :, cols].rearrange("p i (c e) -> p c i e", e=4),
+            )
+
+        def quantize_x(q):
+            nc.vector.quantize_mx(out=x_codes[q][:].bitcast(FP8X4), scales=x_scales[q][:], in_=x_bf[q][:])
+
+        for q in range(4):
+            pick_last_plane(q)
+        weave_x(0)
+        weave_x(1)
+
+        wa_bf = keep.tile([P, PACK * R], BF16, name="wa_bf", align_bytes=64)
+        nc.vector.tensor_copy(
+            wa_bf[:].rearrange("p (t m i) -> p m i t", t=PACK, i=PACK),
+            wa_raw[:].rearrange("p i (m t) -> p m i t", t=PACK),
+        )
+        quantize_x(0)
+        wa_codes = keep.tile([P, R], U32, name="wa_codes", align_bytes=64)
+        wa_plane = keep.tile([P, R], U8, name="wa_plane", align_bytes=64)
+        nc.vector.quantize_mx(out=wa_codes[:].bitcast(FP8X4), scales=wa_plane[:], in_=wa_bf[:])
+        quantize_x(1)
+
+        wb = keep.tile([P, R], I32, name="wb", align_bytes=64)
+        wb_plane = keep.tile([P, R], U8, name="wb_plane", align_bytes=64)
+        nc.vector.tensor_copy(
+            wb[:].rearrange("p (t m) -> p m t", t=PACK), wb_raw[:].rearrange("p (m t) -> p m t", t=PACK)
+        )
+        nc.vector.tensor_copy(
+            wb_plane[:].rearrange("p (t m) -> p m t", t=PACK), wb_plane_raw[:].rearrange("p (m t) -> p m t", t=PACK)
+        )
+
+        out_rows = out.rearrange("(s p) j -> p s j", p=P)
+        chunks = QUARTER // CHUNK
+
+        def gate_of(q):
+            gates = []
+            for c in range(chunks):
+                cols = slice(c * CHUNK, (c + 1) * CHUNK)
+                ya = psum.tile([P, PACK, CHUNK], F32, name="ya", bufs=2)
+                for t in range(PACK):
+                    w_cols = slice(t * P, (t + 1) * P)
+                    product(ya[:, t, :], wa_codes[:, w_cols], wa_plane[:, w_cols], x_codes[q][:, cols], x_scales[q][:, cols])
+                gate = ring.tile([P, CHUNK, PACK], F32, name="gate", bufs=8)
+                nc.scalar.activation(gate[:], ya[:].rearrange("p t j -> p j t"), SILU)
+                gates.append(gate)
+            return gates
+
+        def pick_table(q):
+            v_codes = ring.tile([P, QUARTER], I32, name="v_codes", align_bytes=64)
+            window = tab[:].bitcast(U32).indirect(entries(tab_list, q * QUARTER, QUARTER))
+            nc.vector.tensor_copy(v_codes[:].bitcast(U32), window)
+            return v_codes
+
+        def hidden_of(q, gates, v_codes):
+            h_bf = ring.tile([P, PACK * QUARTER], BF16, name="h_bf", align_bytes=64)
+            for c in range(chunks):
+                cols = slice(c * CHUNK, (c + 1) * CHUNK)
+                list_cols = slice(q * QUARTER + c * CHUNK, q * QUARTER + (c + 1) * CHUNK)
+                yb = psum.tile([P, PACK, CHUNK], F32, name="yb", bufs=2)
+                for t in range(PACK):
+                    w_cols = slice(t * P, (t + 1) * P)
+                    product(yb[:, t, :], wb[:, w_cols], wb_plane[:, w_cols], v_codes[:, cols], v_plane[:, list_cols])
+                h_cols = h_bf[:, c * CHUNK * PACK : (c + 1) * CHUNK * PACK].rearrange("p (j t) -> p j t", t=PACK)
+                nc.vector.tensor_tensor(h_cols, yb[:].rearrange("p t j -> p j t"), gates[c][:], MULT)
+            return h_bf
+
+        def second_layer(h_cols, first, width, copies):
+            h_codes = ring.tile([P, width], U32, name="h_codes", align_bytes=64)
+            h_plane = ring.tile([P, width], U8, name="h_plane", align_bytes=64)
+            nc.vector.quantize_mx(out=h_codes[:].bitcast(FP8X4), scales=h_plane[:], in_=h_cols)
+            y_sb = ring.tile([P, 4, width], F32, name="y_sb", bufs=5)
+            for pair in range(2):
+                y = psum.tile([P, 2, width], F32, name="y", bufs=4)
+                for s in range(2):
+                    w_cols = slice((2 * pair + s) * P, (2 * pair + s + 1) * P)
+                    product(y[:, s, :], wd[:, w_cols], wd_plane[:, w_cols], h_codes[:], h_plane[:])
+                copies[pair](y_sb[:, 2 * pair : 2 * pair + 2, :], y[:])
+                nc.sync.dma_start(out_rows[:, 2 * pair : 2 * pair + 2, first : first + width], y_sb[:, 2 * pair : 2 * pair + 2, :])
+
+        on_scalar = (nc.scalar.copy, nc.scalar.copy)
+        shared = (nc.scalar.copy, nc.vector.tensor_copy)
+
+        gates = [gate_of(0)]
+        weave_x(2)
+        quantize_x(2)
+        gates.append(gate_of(1))
+        weave_x(3)
+        quantize_x(3)
+        picks = [pick_table(0), pick_table(1)]
+        for q in range(4):
+            h_bf = hidden_of(q, gates[q], picks[q])
+            if q + 2 < 4:
+                gates.append(gate_of(q + 2))
+            if q < 3:
+                second_layer(h_bf[:], q * QUARTER, QUARTER, on_scalar)
+            else:
+                second_layer(h_bf[:, 0 : CHUNK * PACK], q * QUARTER, CHUNK, on_scalar)
+                second_layer(h_bf[:, CHUNK * PACK :], q * QUARTER + CHUNK, CHUNK, shared)
+            if q + 2 < 4:
+                picks.append(pick_table(q + 2))

@@ -60,17 +60,13 @@ def tile_list_htabg_glu_none_kernel(
 
         tab_list = keep.tile([P, J // LIST_ROWS], U16, name="tab_list")
         nc.sync.dma_start(tab_list[:], offs)
-        tab_rows = keep.tile([P, T], U8, name="tab_rows", align_bytes=64)
-        nc.sync.dma_start(
-            tab_rows[:].bitcast(I32), tab_scales[0].bitcast(I32).unsqueeze(1).to_broadcast([16, 8, T // 4])
-        )
         head_lists = keep.tile([P, J // LIST_ROWS], U16, name="head_lists")
-        nc.sync.dma_start(head_lists[:], offs2)
+        tab_rows = keep.tile([P, T], U8, name="tab_rows", align_bytes=64)
 
         v_plane = keep.tile([P, J], U8, name="v_plane", align_bytes=64)
         wb_plane_raw = keep.tile([P, R], U8, name="wb_plane_raw", align_bytes=64)
         wd_plane = keep.tile([P, N], U8, name="wd_plane", align_bytes=64)
-        for plane in (v_plane, wb_plane_raw, wd_plane):
+        for plane in (tab_rows, wb_plane_raw, wd_plane):
             nc.gpsimd.memset(plane[:].bitcast(I32), 0)
 
         x_rows = xT.rearrange("(p i) t -> p i t", i=PACK)
@@ -79,21 +75,17 @@ def tile_list_htabg_glu_none_kernel(
         wa_raw = keep.tile([P, PACK, R], F32, name="wa_raw")
 
         nc.sync.dma_start(wgt[0][:], wgt2[:, 0:HALF])
+        load_scale_rows(tab_rows, tab_scales)
+        nc.sync.dma_start(head_lists[:], offs2)
         nc.sync.dma_start(x_planes[0][:], x_rows[:, 0, :])
         nc.sync.dma_start(wgt[1][:], wgt2[:, HALF:J])
-        nc.sync.dma_start(x_planes[1][:], x_rows[:, 1, :])
-        v_rows = keep.tile([P, J], U8, name="v_rows", align_bytes=64)
-        nc.vector.tensor_copy(v_rows[:], tab_rows[:].indirect(tab_list[:]))
         load_scale_rows(wb_plane_raw, wb_scales)
+        nc.sync.dma_start(x_planes[1][:], x_rows[:, 1, :])
+        nc.vector.tensor_copy(v_plane[:], tab_rows[:].indirect(tab_list[:]))
         nc.sync.dma_start(x_planes[2][:], x_rows[:, 2, :])
-        for quad in range(4):
-            nc.sync.dma_start(
-                v_plane[32 * quad : 32 * quad + 4, :].bitcast(I32),
-                v_rows[32 * quad : 32 * quad + 32 : 8, :].bitcast(I32),
-            )
-        wb_raw = load_words("wb_raw", wb_words, R)
         nc.sync.dma_start(x_planes[3][:], x_rows[:, 3, :])
         nc.sync.dma_start(wa_raw[:], wa.rearrange("(p i) r -> p i r", i=PACK))
+        wb_raw = load_words("wb_raw", wb_words, R)
         tab = load_words("tab", tab_words, T)
         wd = load_words("wd", wd_words, N)
         load_scale_rows(wd_plane, wd_scales)
@@ -151,7 +143,7 @@ def tile_list_htabg_glu_none_kernel(
             wb[:].rearrange("p (t m) -> p m t", t=PACK), wb_raw[:].rearrange("p (m t) -> p m t", t=PACK)
         )
         nc.vector.tensor_copy(
-            wb_plane[:].rearrange("p (t m) -> p m t", t=PACK), wb_plane_raw[:].rearrange("p (m t) -> p m t", t=PACK)
+            wb_plane[:].rearrange("p (t m) -> p t m", t=PACK), wb_plane_raw[:].rearrange("p (m t) -> p t m", t=PACK)
         )
 
         out_rows = out.rearrange("(s p) j -> p s j", p=P)
@@ -161,65 +153,65 @@ def tile_list_htabg_glu_none_kernel(
             gates = []
             for c in range(chunks):
                 cols = slice(c * CHUNK, (c + 1) * CHUNK)
-                ya = psum.tile([P, PACK, CHUNK], F32, name="ya", bufs=2)
+                ya = psum.tile([P, PACK, CHUNK], F32, name="ya", tag="acc", bufs=4)
                 for t in range(PACK):
                     w_cols = slice(t * P, (t + 1) * P)
                     product(ya[:, t, :], wa_codes[:, w_cols], wa_plane[:, w_cols], x_codes[q][:, cols], x_scales[q][:, cols])
-                gate = ring.tile([P, CHUNK, PACK], F32, name="gate", bufs=8)
-                nc.scalar.activation(gate[:], ya[:].rearrange("p t j -> p j t"), SILU)
+                gate = ring.tile([P, CHUNK // 2, PACK, 2], F32, name="gate", bufs=8)
+                nc.scalar.activation(gate[:], ya[:].rearrange("p t (c e) -> p c t e", e=2), SILU)
                 gates.append(gate)
             return gates
 
         def pick_table(q):
-            v_codes = ring.tile([P, QUARTER], I32, name="v_codes", align_bytes=64)
+            v_codes = ring.tile([P, QUARTER], I32, name="v_codes", bufs=4, align_bytes=64)
             window = tab[:].bitcast(U32).indirect(entries(tab_list, q * QUARTER, QUARTER))
             nc.vector.tensor_copy(v_codes[:].bitcast(U32), window)
             return v_codes
 
         def hidden_of(q, gates, v_codes):
-            h_bf = ring.tile([P, PACK * QUARTER], BF16, name="h_bf", align_bytes=64)
+            h_bf = ring.tile([P, PACK * QUARTER], BF16, name="h_bf", bufs=3, align_bytes=64)
             for c in range(chunks):
                 cols = slice(c * CHUNK, (c + 1) * CHUNK)
                 list_cols = slice(q * QUARTER + c * CHUNK, q * QUARTER + (c + 1) * CHUNK)
-                yb = psum.tile([P, PACK, CHUNK], F32, name="yb", bufs=2)
+                yb = psum.tile([P, PACK, CHUNK], F32, name="yb", bufs=4)
                 for t in range(PACK):
                     w_cols = slice(t * P, (t + 1) * P)
                     product(yb[:, t, :], wb[:, w_cols], wb_plane[:, w_cols], v_codes[:, cols], v_plane[:, list_cols])
-                h_cols = h_bf[:, c * CHUNK * PACK : (c + 1) * CHUNK * PACK].rearrange("p (j t) -> p j t", t=PACK)
-                nc.vector.tensor_tensor(h_cols, yb[:].rearrange("p t j -> p j t"), gates[c][:], MULT)
+                h_cols = h_bf[:, c * CHUNK * PACK : (c + 1) * CHUNK * PACK].rearrange("p (c e t) -> p c t e", e=2, t=PACK)
+                nc.vector.tensor_tensor(h_cols, yb[:].rearrange("p t (c e) -> p c t e", e=2), gates[c][:], MULT)
             return h_bf
 
         def second_layer(h_cols, first, width, copies):
-            h_codes = ring.tile([P, width], U32, name="h_codes", align_bytes=64)
-            h_plane = ring.tile([P, width], U8, name="h_plane", align_bytes=64)
+            h_codes = ring.tile([P, width], U32, name="h_codes", bufs=3, align_bytes=64)
+            h_plane = ring.tile([P, width], U8, name="h_plane", bufs=3, align_bytes=64)
             nc.vector.quantize_mx(out=h_codes[:].bitcast(FP8X4), scales=h_plane[:], in_=h_cols)
             y_sb = ring.tile([P, 4, width], F32, name="y_sb", bufs=5)
             for pair in range(2):
-                y = psum.tile([P, 2, width], F32, name="y", bufs=4)
+                y = psum.tile([P, 2, width], F32, name="y", tag="acc", bufs=4)
                 for s in range(2):
                     w_cols = slice((2 * pair + s) * P, (2 * pair + s + 1) * P)
                     product(y[:, s, :], wd[:, w_cols], wd_plane[:, w_cols], h_codes[:], h_plane[:])
                 copies[pair](y_sb[:, 2 * pair : 2 * pair + 2, :], y[:])
                 nc.sync.dma_start(out_rows[:, 2 * pair : 2 * pair + 2, first : first + width], y_sb[:, 2 * pair : 2 * pair + 2, :])
 
-        on_scalar = (nc.scalar.copy, nc.scalar.copy)
-        shared = (nc.scalar.copy, nc.vector.tensor_copy)
-
-        gates = [gate_of(0)]
+        g0 = gate_of(0)
         weave_x(2)
         quantize_x(2)
-        gates.append(gate_of(1))
+        g1 = gate_of(1)
         weave_x(3)
         quantize_x(3)
-        picks = [pick_table(0), pick_table(1)]
-        for q in range(4):
-            h_bf = hidden_of(q, gates[q], picks[q])
-            if q + 2 < 4:
-                gates.append(gate_of(q + 2))
-            if q < 3:
-                second_layer(h_bf[:], q * QUARTER, QUARTER, on_scalar)
-            else:
-                second_layer(h_bf[:, 0 : CHUNK * PACK], q * QUARTER, CHUNK, on_scalar)
-                second_layer(h_bf[:, CHUNK * PACK :], q * QUARTER + CHUNK, CHUNK, shared)
-            if q + 2 < 4:
-                picks.append(pick_table(q + 2))
+        v0 = pick_table(0)
+        v1 = pick_table(1)
+        v2 = pick_table(2)
+        v3 = pick_table(3)
+        g2 = gate_of(2)
+        h0 = hidden_of(0, g0, v0)
+        g3 = gate_of(3)
+        second_layer(h0[:], 0 * QUARTER, QUARTER, (nc.scalar.copy, nc.scalar.copy))
+        h1 = hidden_of(1, g1, v1)
+        second_layer(h1[:], 1 * QUARTER, QUARTER, (nc.scalar.copy, nc.scalar.copy))
+        h2 = hidden_of(2, g2, v2)
+        second_layer(h2[:], 2 * QUARTER, QUARTER, (nc.scalar.copy, nc.scalar.copy))
+        h3 = hidden_of(3, g3, v3)
+        second_layer(h3[:, 0 : CHUNK * PACK], 3 * QUARTER, CHUNK, (nc.scalar.copy, nc.vector.tensor_copy))
+        second_layer(h3[:, CHUNK * PACK :], 3 * QUARTER + CHUNK, CHUNK, (nc.scalar.copy, nc.vector.tensor_copy))

@@ -147,71 +147,86 @@ def tile_list_htabg_glu_none_kernel(
         )
 
         out_rows = out.rearrange("(s p) j -> p s j", p=P)
-        chunks = QUARTER // CHUNK
+        segments = [[0,256],[256,256],[512,256],[768,256]]
+        gates = {}
+        picks = {}
+        h_bf = [keep.tile([P, PACK * width], BF16, name="h_bf%d" % n, align_bytes=64) for n, (first, width) in enumerate(segments)]
+        h_codes = [keep.tile([P, width], U32, name="h_codes%d" % n, align_bytes=64) for n, (first, width) in enumerate(segments)]
+        h_plane = [keep.tile([P, width], U8, name="h_plane%d" % n, align_bytes=64) for n, (first, width) in enumerate(segments)]
 
-        def gate_of(q):
-            gates = []
-            for c in range(chunks):
-                cols = slice(c * CHUNK, (c + 1) * CHUNK)
-                ya = psum.tile([P, PACK, CHUNK], F32, name="ya", tag="acc", bufs=4)
-                for t in range(PACK):
-                    w_cols = slice(t * P, (t + 1) * P)
-                    product(ya[:, t, :], wa_codes[:, w_cols], wa_plane[:, w_cols], x_codes[q][:, cols], x_scales[q][:, cols])
-                gate = ring.tile([P, CHUNK // 2, PACK, 2], F32, name="gate", bufs=8)
-                nc.scalar.activation(gate[:], ya[:].rearrange("p t (c e) -> p c t e", e=2), SILU)
-                gates.append(gate)
-            return gates
+        def gate_of(c):
+            q, cols = c // 2, slice((c % 2) * CHUNK, (c % 2 + 1) * CHUNK)
+            ya = psum.tile([P, PACK, CHUNK], F32, name="ya", tag="acc", bufs=4)
+            for t in range(PACK):
+                w_cols = slice(t * P, (t + 1) * P)
+                product(ya[:, t, :], wa_codes[:, w_cols], wa_plane[:, w_cols], x_codes[q][:, cols], x_scales[q][:, cols])
+            gate = ring.tile([P, CHUNK // 2, PACK, 2], F32, name="gate", bufs=8)
+            nc.scalar.activation(gate[:], ya[:].rearrange("p t (c e) -> p c t e", e=2), SILU)
+            gates.setdefault(c, gate)
 
         def pick_table(q):
-            v_codes = ring.tile([P, QUARTER], I32, name="v_codes", bufs=4, align_bytes=64)
-            window = tab[:].bitcast(U32).indirect(entries(tab_list, q * QUARTER, QUARTER))
+            v_codes = ring.tile([P, 256], I32, name="v_codes", bufs=4, align_bytes=64)
+            window = tab[:].bitcast(U32).indirect(entries(tab_list, q * 256, 256))
             nc.vector.tensor_copy(v_codes[:].bitcast(U32), window)
-            return v_codes
+            picks.setdefault(q, v_codes)
 
-        def hidden_of(q, gates, v_codes):
-            h_bf = ring.tile([P, PACK * QUARTER], BF16, name="h_bf", bufs=3, align_bytes=64)
-            for c in range(chunks):
-                cols = slice(c * CHUNK, (c + 1) * CHUNK)
-                list_cols = slice(q * QUARTER + c * CHUNK, q * QUARTER + (c + 1) * CHUNK)
-                yb = psum.tile([P, PACK, CHUNK], F32, name="yb", bufs=4)
-                for t in range(PACK):
-                    w_cols = slice(t * P, (t + 1) * P)
-                    product(yb[:, t, :], wb[:, w_cols], wb_plane[:, w_cols], v_codes[:, cols], v_plane[:, list_cols])
-                h_cols = h_bf[:, c * CHUNK * PACK : (c + 1) * CHUNK * PACK].rearrange("p (c e t) -> p c t e", e=2, t=PACK)
-                nc.vector.tensor_tensor(h_cols, yb[:].rearrange("p t (c e) -> p c t e", e=2), gates[c][:], MULT)
-            return h_bf
+        def hidden_of(c):
+            q, at = divmod(c * CHUNK, 256)
+            cols = slice(at, at + CHUNK)
+            list_cols = slice(c * CHUNK, (c + 1) * CHUNK)
+            yb = psum.tile([P, PACK, CHUNK], F32, name="yb", tag="yb", bufs=4)
+            for t in range(PACK):
+                w_cols = slice(t * P, (t + 1) * P)
+                product(yb[:, t, :], wb[:, w_cols], wb_plane[:, w_cols], picks[q][:, cols], v_plane[:, list_cols])
+            n = max(n for n, (first, width) in enumerate(segments) if first <= c * CHUNK)
+            col = (c * CHUNK - segments[n][0]) * PACK
+            h_cols = h_bf[n][:, col : col + CHUNK * PACK].rearrange("p (c e t) -> p c t e", e=2, t=PACK)
+            nc.vector.tensor_tensor(h_cols, yb[:].rearrange("p t (c e) -> p c t e", e=2), gates[c][:], MULT)
 
-        def second_layer(h_cols, first, width, copies):
-            h_codes = ring.tile([P, width], U32, name="h_codes", bufs=3, align_bytes=64)
-            h_plane = ring.tile([P, width], U8, name="h_plane", bufs=3, align_bytes=64)
-            nc.vector.quantize_mx(out=h_codes[:].bitcast(FP8X4), scales=h_plane[:], in_=h_cols)
-            y_sb = ring.tile([P, 4, width], F32, name="y_sb", bufs=5)
-            for pair in range(2):
-                y = psum.tile([P, 2, width], F32, name="y", tag="acc", bufs=4)
-                for s in range(2):
-                    w_cols = slice((2 * pair + s) * P, (2 * pair + s + 1) * P)
-                    product(y[:, s, :], wd[:, w_cols], wd_plane[:, w_cols], h_codes[:], h_plane[:])
-                copies[pair](y_sb[:, 2 * pair : 2 * pair + 2, :], y[:])
-                nc.sync.dma_start(out_rows[:, 2 * pair : 2 * pair + 2, first : first + width], y_sb[:, 2 * pair : 2 * pair + 2, :])
+        def quantize_h(n):
+            nc.vector.quantize_mx(out=h_codes[n][:].bitcast(FP8X4), scales=h_plane[n][:], in_=h_bf[n][:])
 
-        g0 = gate_of(0)
+        def second_layer(n, copies):
+            first, width = segments[n]
+            blocks = 4 // len(copies)
+            for part, copy in enumerate(copies):
+                y = psum.tile([P, blocks, width], F32, name="y", tag="acc", bufs=4)
+                for s in range(blocks):
+                    w_cols = slice((blocks * part + s) * P, (blocks * part + s + 1) * P)
+                    product(y[:, s, :], wd[:, w_cols], wd_plane[:, w_cols], h_codes[n][:], h_plane[n][:])
+                y_sb = keep.tile([P, blocks, width], F32, name="y_sb%d_%d" % (n, part))
+                copy(y_sb[:], y[:])
+                nc.sync.dma_start(out_rows[:, blocks * part : blocks * (part + 1), first : first + width], y_sb[:])
+
+        gate_of(0)
+        gate_of(1)
         weave_x(2)
         quantize_x(2)
-        g1 = gate_of(1)
+        gate_of(2)
+        gate_of(3)
         weave_x(3)
         quantize_x(3)
-        v0 = pick_table(0)
-        v1 = pick_table(1)
-        v2 = pick_table(2)
-        v3 = pick_table(3)
-        g2 = gate_of(2)
-        h0 = hidden_of(0, g0, v0)
-        g3 = gate_of(3)
-        second_layer(h0[:], 0 * QUARTER, QUARTER, (nc.scalar.copy, nc.scalar.copy))
-        h1 = hidden_of(1, g1, v1)
-        second_layer(h1[:], 1 * QUARTER, QUARTER, (nc.scalar.copy, nc.scalar.copy))
-        h2 = hidden_of(2, g2, v2)
-        second_layer(h2[:], 2 * QUARTER, QUARTER, (nc.scalar.copy, nc.scalar.copy))
-        h3 = hidden_of(3, g3, v3)
-        second_layer(h3[:, 0 : CHUNK * PACK], 3 * QUARTER, CHUNK, (nc.scalar.copy, nc.vector.tensor_copy))
-        second_layer(h3[:, CHUNK * PACK :], 3 * QUARTER + CHUNK, CHUNK, (nc.scalar.copy, nc.vector.tensor_copy))
+        pick_table(0)
+        pick_table(1)
+        pick_table(2)
+        pick_table(3)
+        gate_of(4)
+        gate_of(5)
+        hidden_of(0)
+        hidden_of(1)
+        gate_of(6)
+        gate_of(7)
+        quantize_h(0)
+        second_layer(0, [nc.scalar.copy, nc.scalar.copy])
+        hidden_of(2)
+        hidden_of(3)
+        quantize_h(1)
+        second_layer(1, [nc.scalar.copy, nc.scalar.copy])
+        hidden_of(4)
+        hidden_of(5)
+        quantize_h(2)
+        second_layer(2, [nc.scalar.copy, nc.scalar.copy])
+        hidden_of(6)
+        hidden_of(7)
+        quantize_h(3)
+        second_layer(3, [nc.scalar.copy, nc.vector.tensor_copy, nc.scalar.copy, nc.vector.tensor_copy])

@@ -190,7 +190,7 @@ def tile_list_htabg_glu_none_kernel(
             first, width = segments[n]
             blocks = 4 // len(copies)
             for part, copy in enumerate(copies):
-                y = psum.tile([P, blocks, width], F32, name="y", tag="acc", bufs=4)
+                y = psum.tile([P, blocks, width], F32, name="y", tag="yb" if n == len(segments) - 1 else "acc", bufs=4)
                 for s in range(blocks):
                     w_cols = slice((blocks * part + s) * P, (blocks * part + s + 1) * P)
                     product(y[:, s, :], wd[:, w_cols], wd_plane[:, w_cols], h_codes[n][:], h_plane[n][:])
@@ -217,15 +217,15 @@ def tile_list_htabg_glu_none_kernel(
         gate_of(6)
         gate_of(7)
         quantize_h(0)
-        second_layer(0, [nc.scalar.copy, nc.scalar.copy])
+        second_layer(0, [nc.scalar.copy, nc.scalar.copy, nc.scalar.copy, nc.scalar.copy])
         hidden_of(2)
         hidden_of(3)
         quantize_h(1)
-        second_layer(1, [nc.scalar.copy, nc.scalar.copy])
+        second_layer(1, [nc.scalar.copy, nc.scalar.copy, nc.scalar.copy, nc.scalar.copy])
         hidden_of(4)
         hidden_of(5)
         quantize_h(2)
-        second_layer(2, [nc.scalar.copy, nc.scalar.copy])
+        second_layer(2, [nc.scalar.copy, nc.scalar.copy, nc.scalar.copy, nc.scalar.copy])
         hidden_of(6)
         hidden_of(7)
         quantize_h(3)

from contextlib import ExitStack

import concourse.mybir as mybir

K, L, R, N, T, J = 512, 512, 512, 512, 2048, 1024
FLOPS = 2 * J * (K * R + L * R + R * N)

F32 = mybir.dt.float32
BF16 = mybir.dt.bfloat16
I32 = mybir.dt.int32
U32 = mybir.dt.uint32
U16 = mybir.dt.uint16
U8 = mybir.dt.uint8
FP8X4 = mybir.dt.float8_e4m3fn_x4
MULT = mybir.AluOpType.mult
SILU = mybir.ActivationFunctionType.Silu

P = 128
PACK = 4
LIST_ROWS = 16
HALF = J // 2
QUARTER = J // 4
CHUNK = 128


def tile_list_htabg_glu_none_kernel(
    tc, tab_words, tab_scales, xT, wgt2, wa, wb_words, wb_scales, wd_words, wd_scales, offs, offs2, out
):
    nc = tc.nc
    with ExitStack() as ctx:
        keep = ctx.enter_context(tc.tile_pool(name="keep", bufs=1))
        ring = ctx.enter_context(tc.tile_pool(name="ring", bufs=2))
        psum = ctx.enter_context(tc.psum_pool(name="psum", bufs=2))

        def load_scale_rows(plane, rows):
            for quad in range(4):
                nc.sync.dma_start(
                    plane[32 * quad : 32 * quad + 4, :].bitcast(I32),
                    rows[0, 4 * quad : 4 * quad + 4, :].bitcast(I32),
                )

        def load_words(name, words, width):
            tile = keep.tile([P, width], I32, name=name, align_bytes=64)
            nc.sync.dma_start(tile[:], words[0].rearrange("p n t -> p (n t)").bitcast(I32))
            return tile

        def entries(offsets, first, count):
            return offsets[:, first // LIST_ROWS : (first + count) // LIST_ROWS]

        def product(acc, w_codes, w_plane, codes, plane):
            nc.tensor.matmul_mx(
                out=acc,
                lhsT=w_codes.bitcast(FP8X4),
                lhsT_scale=w_plane,
                rhs=codes.bitcast(FP8X4),
                rhs_scale=plane,
                start=True,
                stop=True,
            )

        tab_list = keep.tile([P, J // LIST_ROWS], U16, name="tab_list")
        nc.sync.dma_start(tab_list[:], offs)
        head_lists = keep.tile([P, J // LIST_ROWS], U16, name="head_lists")
        tab_rows = keep.tile([P, T], U8, name="tab_rows", align_bytes=64)

        v_plane = keep.tile([P, J], U8, name="v_plane", align_bytes=64)
        wb_plane_raw = keep.tile([P, R], U8, name="wb_plane_raw", align_bytes=64)
        wd_plane = keep.tile([P, N], U8, name="wd_plane", align_bytes=64)
        for plane in (tab_rows, wb_plane_raw, wd_plane):
            nc.gpsimd.memset(plane[:].bitcast(I32), 0)

        x_rows = xT.rearrange("(p i) t -> p i t", i=PACK)
        x_planes = [keep.tile([P, T], F32, name="x_plane%d" % i) for i in range(PACK)]
        wgt = [keep.tile([P, HALF], F32, name="wgt%d" % h) for h in range(2)]
        wa_raw = keep.tile([P, PACK, R], F32, name="wa_raw")

        nc.sync.dma_start(wgt[0][:], wgt2[:, 0:HALF])
        load_scale_rows(tab_rows, tab_scales)
        nc.sync.dma_start(head_lists[:], offs2)
        nc.sync.dma_start(x_planes[0][:], x_rows[:, 0, :])
        nc.sync.dma_start(wgt[1][:], wgt2[:, HALF:J])
        load_scale_rows(wb_plane_raw, wb_scales)
        nc.sync.dma_start(x_planes[1][:], x_rows[:, 1, :])
        nc.vector.tensor_copy(v_plane[:], tab_rows[:].indirect(tab_list[:]))
        nc.sync.dma_start(x_planes[2][:], x_rows[:, 2, :])
        nc.sync.dma_start(x_planes[3][:], x_rows[:, 3, :])
        nc.sync.dma_start(wa_raw[:], wa.rearrange("(p i) r -> p i r", i=PACK))
        wb_raw = load_words("wb_raw", wb_words, R)
        tab = load_words("tab", tab_words, T)
        wd = load_words("wd", wd_words, N)
        load_scale_rows(wd_plane, wd_scales)

        warm = keep.tile([P, 1], F32, name="warm")
        nc.scalar.activation(warm[:], wgt[0][:, 0:1], SILU)

        picked = [keep.tile([P, PACK, HALF], F32, name="picked%d" % h) for h in range(2)]
        for i in range(PACK - 1):
            for h in range(2):
                window = x_planes[i][:].indirect(entries(head_lists, h * HALF, HALF))
                nc.vector.tensor_tensor(picked[h][:, i, :], window, wgt[h][:], MULT)

        x_codes = [keep.tile([P, QUARTER], U32, name="x_codes%d" % q, align_bytes=64) for q in range(4)]
        x_scales = [keep.tile([P, QUARTER], U8, name="x_scales%d" % q, align_bytes=64) for q in range(4)]
        x_bf = [keep.tile([P, PACK * QUARTER], BF16, name="x_bf%d" % q, align_bytes=64) for q in range(4)]

        def quarter_cols(q):
            return q // 2, slice((q % 2) * QUARTER, (q % 2 + 1) * QUARTER)

        def pick_last_plane(q):
            h, cols = quarter_cols(q)
            window = x_planes[PACK - 1][:].indirect(entries(head_lists, q * QUARTER, QUARTER))
            nc.vector.tensor_tensor(picked[h][:, PACK - 1, cols], window, wgt[h][:, cols], MULT)

        def weave_x(q):
            h, cols = quarter_cols(q)
            nc.scalar.copy(
                x_bf[q][:].rearrange("p (c e i) -> p c i e", e=4, i=PACK),
                picked[h][:, :, cols].rearrange("p i (c e) -> p c i e", e=4),
            )

        def quantize_x(q):
            nc.vector.quantize_mx(out=x_codes[q][:].bitcast(FP8X4), scales=x_scales[q][:], in_=x_bf[q][:])

        for q in range(4):
            pick_last_plane(q)
        weave_x(0)
        weave_x(1)

        wa_bf = keep.tile([P, PACK * R], BF16, name="wa_bf", align_bytes=64)
        nc.vector.tensor_copy(
            wa_bf[:].rearrange("p (t m i) -> p m i t", t=PACK, i=PACK),
            wa_raw[:].rearrange("p i (m t) -> p m i t", t=PACK),
        )
        quantize_x(0)
        wa_codes = keep.tile([P, R], U32, name="wa_codes", align_bytes=64)
        wa_plane = keep.tile([P, R], U8, name="wa_plane", align_bytes=64)
        nc.vector.quantize_mx(out=wa_codes[:].bitcast(FP8X4), scales=wa_plane[:], in_=wa_bf[:])
        quantize_x(1)

        wb = keep.tile([P, R], I32, name="wb", align_bytes=64)
        wb_plane = keep.tile([P, R], U8, name="wb_plane", align_bytes=64)
        nc.vector.tensor_copy(
            wb[:].rearrange("p (t m) -> p m t", t=PACK), wb_raw[:].rearrange("p (m t) -> p m t", t=PACK)
        )
        nc.vector.tensor_copy(
            wb_plane[:].rearrange("p (t m) -> p t m", t=PACK), wb_plane_raw[:].rearrange("p (m t) -> p t m", t=PACK)
        )

        out_rows = out.rearrange("(s p) j -> p s j", p=P)
        segments = [[0,256],[256,256],[512,256],[768,256]]
        gates = {}
        picks = {}
        h_bf = [keep.tile([P, PACK * width], BF16, name="h_bf%d" % n, align_bytes=64) for n, (first, width) in enumerate(segments)]
        h_codes = [keep.tile([P, width], U32, name="h_codes%d" % n, align_bytes=64) for n, (first, width) in enumerate(segments)]
        h_plane = [keep.tile([P, width], U8, name="h_plane%d" % n, align_bytes=64) for n, (first, width) in enumerate(segments)]

        def gate_of(c):
            q, cols = c // 2, slice((c % 2) * CHUNK, (c % 2 + 1) * CHUNK)
            ya = psum.tile([P, PACK, CHUNK], F32, name="ya", tag="acc", bufs=4)
            for t in range(PACK):
                w_cols = slice(t * P, (t + 1) * P)
                product(ya[:, t, :], wa_codes[:, w_cols], wa_plane[:, w_cols], x_codes[q][:, cols], x_scales[q][:, cols])
            gate = ring.tile([P, CHUNK // 2, PACK, 2], F32, name="gate", bufs=8)
            nc.scalar.activation(gate[:], ya[:].rearrange("p t (c e) -> p c t e", e=2), SILU)
            gates.setdefault(c, gate)

        def pick_table(q):
            v_codes = ring.tile([P, 256], I32, name="v_codes", bufs=4, align_bytes=64)
            window = tab[:].bitcast(U32).indirect(entries(tab_list, q * 256, 256))
            nc.vector.tensor_copy(v_codes[:].bitcast(U32), window)
            picks.setdefault(q, v_codes)

        def hidden_of(c):
            q, at = divmod(c * CHUNK, 256)
            cols = slice(at, at + CHUNK)
            list_cols = slice(c * CHUNK, (c + 1) * CHUNK)
            yb = psum.tile([P, PACK, CHUNK], F32, name="yb", tag="yb", bufs=4)
            for t in range(PACK):
                w_cols = slice(t * P, (t + 1) * P)
                product(yb[:, t, :], wb[:, w_cols], wb_plane[:, w_cols], picks[q][:, cols], v_plane[:, list_cols])
            n = max(n for n, (first, width) in enumerate(segments) if first <= c * CHUNK)
            col = (c * CHUNK - segments[n][0]) * PACK
            h_cols = h_bf[n][:, col : col + CHUNK * PACK].rearrange("p (c e t) -> p c t e", e=2, t=PACK)
            nc.vector.tensor_tensor(h_cols, yb[:].rearrange("p t (c e) -> p c t e", e=2), gates[c][:], MULT)

        def quantize_h(n):
            nc.vector.quantize_mx(out=h_codes[n][:].bitcast(FP8X4), scales=h_plane[n][:], in_=h_bf[n][:])

        def second_layer(n, copies):
            first, width = segments[n]
            blocks = 4 // len(copies)
            for part, copy in enumerate(copies):
                y = psum.tile([P, blocks, width], F32, name="y", tag="yb" if n == len(segments) - 1 else "acc", bufs=4)
                for s in range(blocks):
                    w_cols = slice((blocks * part + s) * P, (blocks * part + s + 1) * P)
                    product(y[:, s, :], wd[:, w_cols], wd_plane[:, w_cols], h_codes[n][:], h_plane[n][:])
                y_sb = keep.tile([P, blocks, width], F32, name="y_sb%d_%d" % (n, part))
                copy(y_sb[:], y[:])
                nc.sync.dma_start(out_rows[:, blocks * part : blocks * (part + 1), first : first + width], y_sb[:])

        gate_of(0)
        gate_of(1)
        weave_x(2)
        quantize_x(2)
        gate_of(2)
        gate_of(3)
        weave_x(3)
        quantize_x(3)
        pick_table(0)
        pick_table(1)
        pick_table(2)
        pick_table(3)
        gate_of(4)
        gate_of(5)
        hidden_of(0)
        hidden_of(1)
        gate_of(6)
        gate_of(7)
        quantize_h(0)
        second_layer(0, [nc.scalar.copy, nc.scalar.copy, nc.scalar.copy, nc.scalar.copy])
        hidden_of(2)
        hidden_of(3)
        quantize_h(1)
        second_layer(1, [nc.scalar.copy, nc.scalar.copy, nc.scalar.copy, nc.scalar.copy])
        hidden_of(4)
        hidden_of(5)
        quantize_h(2)
        second_layer(2, [nc.scalar.copy, nc.scalar.copy, nc.scalar.copy, nc.scalar.copy])
        hidden_of(6)
        hidden_of(7)
        quantize_h(3)
        second_layer(3, [nc.scalar.copy, nc.vector.tensor_copy, nc.scalar.copy, nc.vector.tensor_copy])
